import numpy as np
import ml_dtypes


def mxq(x, axis, fmt="e4m3"):
    dtype, down = {"e4m3": (ml_dtypes.float8_e4m3fn, 7), "e5m2": (ml_dtypes.float8_e5m2, 14)}[fmt]
    v = np.moveaxis(np.asarray(x, np.float32).astype(ml_dtypes.bfloat16).astype(np.float64), axis, -1)
    blocks = v.reshape(v.shape[:-1] + (-1, 32))
    amax = np.abs(blocks).max(-1, keepdims=True)
    byte = np.maximum(np.where(amax > 0, np.frexp(amax)[1] - 1 + 127, 0) - down, 1)
    scale = np.exp2(byte - 127.0)
    codes = (blocks / scale).astype(np.float32).astype(dtype).astype(np.float64)
    return np.moveaxis((codes * scale).reshape(v.shape), -1, axis)


WIDE = False


def mx_kscale(k):
    if not WIDE:
        return np.ones(k)
    levels = np.array([10, -10, 5, -5, 0])
    if k % 512:
        return np.exp2(np.random.permutation(np.resize(levels, k // 32))).repeat(32)
    a = np.empty((k // 512, 16))
    for p in range(k // 512):
        a[p, :8] = np.random.permutation(np.resize(levels, 8))
        for g in range(8):
            far = levels[np.abs(levels - a[p, g]) >= 10]
            a[p, g + 8] = far[np.random.randint(len(far))]
    return np.exp2(a.ravel()).repeat(32)


def f64(x):
    return np.asarray(x).astype(np.float64)


def striped(idx):
    return np.tile(idx.reshape(-1, 16).T, (8, 1)).astype(np.uint16)


def unstriped(offs):
    return offs[:16].T.reshape(-1).astype(np.int64)


def striped8(idx):
    return np.concatenate([x.reshape(-1, 16).T for x in idx]).astype(np.uint16)


def runs(offs, k):
    lists = np.stack([offs[16 * r : 16 * r + 16].T.reshape(-1) for r in range(8)]).astype(np.int64)
    return lists[np.arange(k) % 512 // 64]


def pack_weight(w):
    k, n = w.shape
    w = f64(np.asarray(w, np.float32).astype(ml_dtypes.bfloat16)).reshape(k // 32, 32, n)
    amax = np.abs(w).max(1)
    byte = np.clip(np.where(amax > 0, np.frexp(amax)[1] - 1 + 127 - 7, 1), 1, 254)
    scaled = (w * np.exp2(127.0 - byte)[:, None, :]).reshape(k, n).astype(np.float32)
    words = np.ascontiguousarray(scaled.reshape(k // 512, 128, 4, n).transpose(0, 1, 3, 2)).astype(ml_dtypes.float8_e4m3fn).view(np.uint8)
    return words, np.ascontiguousarray(byte.astype(np.uint8).reshape(k // 512, 16, n))


def unpack_weight(words, scales):
    g, p, n, _ = words.shape
    vals = np.ascontiguousarray(words).view(ml_dtypes.float8_e4m3fn).astype(np.float64) * np.repeat(np.exp2(scales.astype(np.float64) - 127.0), 8, axis=1)[..., None]
    return vals.transpose(0, 1, 3, 2).reshape(g * 512, n)


E2M1 = np.array([0.0, 0.5, 1.0, 1.5, 2.0, 3.0, 4.0, 6.0, -0.0, -0.5, -1.0, -1.5, -2.0, -3.0, -4.0, -6.0])


def pack_fp4(w):
    k, n = w.shape
    w = f64(np.asarray(w, np.float32).astype(ml_dtypes.bfloat16)).reshape(k // 32, 32, n)
    amax = np.abs(w).max(1)
    mant, ex = np.frexp(amax / 6.0)
    byte = np.clip(np.where(amax > 0, np.where(mant > 0.5, ex, ex - 1) + 127, 1), 1, 254)
    scaled = (w * np.exp2(127.0 - byte)[:, None, :]).reshape(k, n).astype(np.float32)
    c = np.ascontiguousarray(scaled.reshape(k // 512, 128, 4, n).transpose(0, 1, 3, 2)).astype(ml_dtypes.float4_e2m1fn).view(np.uint8) & 0xF
    words = (c[..., 0::2] | (c[..., 1::2] << 4)).reshape(k // 512, 128, 2 * n)
    return np.ascontiguousarray(words), np.ascontiguousarray(byte.astype(np.uint8).reshape(k // 512, 16, n))


def unpack_fp4(words, scales):
    g, _, n = scales.shape
    words = np.ascontiguousarray(words).reshape(g, 128, n, 2)
    nib = np.empty((g, 128, n, 4), np.uint8)
    nib[..., 0::2] = words & 0xF
    nib[..., 1::2] = words >> 4
    vals = E2M1[nib] * np.repeat(np.exp2(scales.astype(np.float64) - 127.0), 8, axis=1)[..., None]
    return vals.transpose(0, 1, 3, 2).reshape(g * 512, n)


def planes(y):
    n, m = y.shape
    v = y.astype(np.float32).astype(ml_dtypes.bfloat16).astype(np.float64).reshape(n // 32, 32, m)
    top = np.abs(v).max(1)
    byte = np.clip(np.where(top > 0, np.frexp(top)[1] - 1 + 127 - 7, 1), 1, 254)
    codes = (v * np.exp2(127.0 - byte)[:, None, :]).reshape(n, m).astype(np.float32).astype(ml_dtypes.float8_e4m3fn).view(np.uint8)
    words = codes.reshape(n // 512, 128, 4, m).transpose(0, 1, 3, 2)
    return np.ascontiguousarray(words), np.ascontiguousarray(byte.astype(np.uint8).reshape(n // 512, 16, m))


K, T, S, H, G, U = 512, 1024, 512, 512, 2048, 1024


def setup_inputs():
    n = np.random.standard_normal
    s = mx_kscale(K)[:, None]
    packed_xT = pack_weight(n((K, T)) * s)
    packed_w1 = pack_fp4(n((K, H)) / np.sqrt(K) / s)
    packed_w2 = pack_fp4(n((K, H)) / np.sqrt(K) / s)
    packed_dT = pack_weight(n((K, G)) / s)
    return {
        "x_words": packed_xT[0],
        "x_scales": packed_xT[1],
        "w1_words": packed_w1[0],
        "w1_scales": packed_w1[1],
        "w2_words": packed_w2[0],
        "w2_scales": packed_w2[1],
        "gs": (np.random.uniform(0.5, 1.5, (K, 1)) * s).astype(np.float32),
        "d_words": packed_dT[0],
        "d_scales": packed_dT[1],
        "mem": n((H, U)).astype(np.float32),
        "offs": striped(np.random.permutation(T)[:S]),
        "two": striped(np.random.permutation(T)[:S]),
        "n1": striped8(np.stack([np.random.permutation(S) for _ in range(8)])),
        "n2": striped8(np.stack([np.random.permutation(S) for _ in range(8)])),
        "n3": striped8(np.stack([np.random.permutation(S) for _ in range(8)])),
        "k1": striped8(np.random.randint(0, G, (8, H))),
        "n4": striped8(np.stack([np.random.permutation(U)[:S] for _ in range(8)])),
    }


def reference(x_words, x_scales, w1_words, w1_scales, w2_words, w2_scales, gs, d_words, d_scales, mem, offs, two, n1, n2, n3, k1, n4):
    d_k1 = unpack_weight(d_words, d_scales)[np.arange(K)[:, None], runs(k1, K)]
    xq = unpack_weight(x_words, x_scales)[:, unstriped(offs)]
    y = unpack_fp4(w1_words, w1_scales).T @ xq
    x_two = unpack_weight(x_words, x_scales)[:, unstriped(two)]
    d = unpack_fp4(w2_words, w2_scales).T @ x_two
    z = f64(gs) * (np.maximum(np.minimum(y - (0.5 * (y[np.arange(H)[:, None], runs(n1, H)])), d[np.arange(H)[:, None], runs(n2, H)]), d[np.arange(H)[:, None], runs(n3, H)]))
    h = 0.0625 * ((d_k1.T @ mxq(z, 0, "e4m3")))
    out = f64(mem).copy()
    out[np.arange(H)[:, None], runs(n4, H)] = h
    return (out,) + planes(out)

@@ -1,0 +1,241 @@
+from contextlib import ExitStack
+
+import concourse.mybir as mybir
+
+K, T, S, H, G, U = 512, 1024, 512, 512, 2048, 1024
+FLOPS = 3 * 2 * 512 * 512 * 512
+
+F32 = mybir.dt.float32
+BF16 = mybir.dt.bfloat16
+I32 = mybir.dt.int32
+U32 = mybir.dt.uint32
+U16 = mybir.dt.uint16
+U8 = mybir.dt.uint8
+FP8X4 = mybir.dt.float8_e4m3fn_x4
+FP4X4 = mybir.dt.float4_e2m1fn_x4
+ALU = mybir.AluOpType
+COPY = mybir.ActivationFunctionType.Copy
+
+P = 128
+PACK = 4
+PIECES = ((0, 256), (256, 384), (384, 512))
+HALF = U // 2
+FIRST, LAST = 2, 3
+ORDER = (FIRST, 0, 1, LAST)
+
+
+def tile_picked_twqclampbpage_none_po_kernel(
+    tc, x_words, x_scales, w1_words, w1_scales, w2_words, w2_scales, gs, d_words, d_scales, mem,
+    offs, two, n1, n2, n3, k1, n4, out_0, out_1, out_2,
+):
+    nc = tc.nc
+    with ExitStack() as ctx:
+        keep = ctx.enter_context(tc.tile_pool(name="keep", bufs=1))
+        psum = ctx.enter_context(tc.psum_pool(name="psum", bufs=1))
+
+        def sb(name, shape, dtype):
+            return keep.tile(shape, dtype, name=name, align_bytes=64)
+
+        def load_list(name, src):
+            tile = keep.tile([P, S // 16], U16, name=name)
+            nc.sync.dma_start(tile[:], src)
+            return tile
+
+        def zeroed_bytes(name, width):
+            tile = sb(name, [P, width], U8)
+            nc.vector.memset(tile[:].bitcast(I32), 0)
+            return tile
+
+        def load_plane(tile, src):
+            rows = src[0].bitcast(I32)
+            for q in range(4):
+                nc.sync.dma_start(tile[32 * q : 32 * q + 4, :].bitcast(I32), rows[4 * q : 4 * q + 4, :])
+
+        def entries(lst, lo, hi):
+            return lst[:, lo // 16 : hi // 16]
+
+        xs = zeroed_bytes("xs", T)
+        w1s = zeroed_bytes("w1s", H)
+        w2s = zeroed_bytes("w2s", H)
+        ds = zeroed_bytes("ds", G)
+        dk_plane = zeroed_bytes("dk_plane", H)
+
+        w1w = sb("w1w", [P, 2 * H], U8)
+        nc.sync.dma_start(w1w[:].bitcast(I32), w1_words[0].bitcast(I32))
+        offs_t = load_list("offs_t", offs)
+        xw = sb("xw", [P, T], U32)
+        nc.sync.dma_start(xw[:].bitcast(I32), x_words[0].rearrange("p c r -> p (c r)").bitcast(I32))
+        load_plane(xs, x_scales)
+        w2w = sb("w2w", [P, 2 * H], U8)
+        nc.sync.dma_start(w2w[:].bitcast(I32), w2_words[0].bitcast(I32))
+        two_t = load_list("two_t", two)
+        load_plane(w1s, w1_scales)
+        load_plane(w2s, w2_scales)
+        k1_t = load_list("k1_t", k1)
+        dw = sb("dw", [P, G], U32)
+        nc.sync.dma_start(dw[:].bitcast(I32), d_words[0].rearrange("p c r -> p (c r)").bitcast(I32))
+        d_rows = d_scales[0].bitcast(I32)
+        for e in range(2):
+            nc.sync.dma_start(ds[e:P:16, :].bitcast(I32), d_rows[e:16:2, :])
+        n1_t = load_list("n1_t", n1)
+        n2_t = load_list("n2_t", n2)
+        n3_t = load_list("n3_t", n3)
+        gs_t = sb("gs_t", [P, PACK], F32)
+        nc.sync.dma_start(gs_t[:], gs.rearrange("(p t) o -> p (t o)", t=PACK))
+        n4_t = load_list("n4_t", n4)
+        mem_rows = mem.rearrange("(p t) w -> p t w", t=PACK)
+        page = []
+        for t in range(PACK):
+            tile = sb(f"page{t}", [P, U], F32)
+            nc.sync.dma_start(tile[:], mem_rows[:, t, :])
+            page.append(tile)
+
+        def deal(name, src, dtype, per_column):
+            dst = sb(name, [P, H * per_column], dtype)
+            if per_column == 1:
+                nc.vector.tensor_copy(
+                    dst[:].rearrange("p (t m) -> p m t", t=PACK), src[:].rearrange("p (m t) -> p m t", t=PACK))
+            else:
+                nc.vector.tensor_copy(
+                    dst[:].rearrange("p (t m b) -> p m t b", t=PACK, b=per_column),
+                    src[:].rearrange("p (m t b) -> p m t b", t=PACK, b=per_column))
+            return dst
+
+        def pick(name, table, lst, dtype):
+            dst = sb(name, [P, S], dtype)
+            nc.vector.tensor_copy(dst[:], table[:].indirect(lst[:]))
+            return dst
+
+        def project(tag, w_codes, w_plane, lst):
+            w_dealt = deal(tag + "_wd", w_codes, U8, 2)
+            codes = pick(tag + "_xw", xw, lst, U32)
+            plane = pick(tag + "_xs", xs, lst, U8)
+            s_dealt = deal(tag + "_sd", w_plane, U8, 1)
+            banks = []
+            for t in range(PACK):
+                bank = psum.tile([P, S], F32, name=f"{tag}_bank{t}", tag=f"{tag}{t}")
+                nc.tensor.matmul_mx(
+                    out=bank[:],
+                    lhsT=w_dealt[:, 2 * P * t : 2 * P * (t + 1)].bitcast(FP4X4),
+                    lhsT_scale=s_dealt[:, P * t : P * (t + 1)],
+                    rhs=codes[:].bitcast(FP8X4),
+                    rhs_scale=plane[:],
+                    start=True, stop=True,
+                )
+                banks.append(bank)
+            return banks
+
+        y, y_half, d = [], [], []
+        for t, bank in enumerate(project("y", w1w, w1s, offs_t)):
+            y_half.append(sb(f"y_half{t}", [P, S], F32))
+            nc.scalar.activation(y_half[t][:], bank[:], COPY, scale=-0.5)
+            y.append(sb(f"y{t}", [P, S], F32))
+            nc.scalar.copy(y[t][:], bank[:])
+        for t, bank in enumerate(project("d", w2w, w2s, two_t)):
+            d.append(sb(f"d{t}", [P, S], F32))
+            nc.scalar.copy(d[t][:], bank[:])
+
+        dk_bytes = pick("dk_bytes", ds, k1_t, U8)
+        dk_words = pick("dk_words", dw, k1_t, U32)
+        dk_bytes_dealt = deal("dk_bytes_dealt", dk_bytes, U8, 1)
+        dk_codes = deal("dk_codes", dk_words, U32, 1)
+        for r in range(4):
+            first = 16 * (r // 2) + r % 2
+            nc.sync.dma_start(dk_plane[r:P:32, :].bitcast(I32), dk_bytes_dealt[first:P:32, :].bitcast(I32))
+
+        h = {t: keep.tile([P, S], F32, name=f"h{t}", tag=f"h{t}", align_bytes=64) for t in ORDER[:-1]}
+        early = [psum.tile([P, S], F32, name=f"early{t}", tag=f"y{t}") for t in range(PACK)]
+        late = [psum.tile([P, S], F32, name=f"late{t}", tag=f"d{t}") for t in range(PACK - 1)] + [early[LAST]]
+        z_in = {}
+
+        def lower_part(i):
+            lo, hi = PIECES[i]
+            n = hi - lo
+            a = sb(f"a{i}", [P, PACK, n], F32)
+            b = sb(f"b{i}", [P, PACK, n], F32)
+            for t in range(PACK):
+                nc.vector.tensor_tensor(a[:, t, :], y_half[t][:].indirect(entries(n1_t, lo, hi)), y[t][:, lo:hi], ALU.add)
+            for t in range(PACK):
+                nc.vector.tensor_copy(b[:, t, :], d[t][:].indirect(entries(n2_t, lo, hi)))
+            return a, b
+
+        def upper_part(i, a, b):
+            lo, hi = PIECES[i]
+            n = hi - lo
+            low = sb(f"low{i}", [P, PACK, n], F32)
+            c = sb(f"c{i}", [P, PACK, n], F32)
+            top = sb(f"top{i}", [P, PACK, n], F32)
+            nc.vector.tensor_copy(c[:, 0, :], d[0][:].indirect(entries(n3_t, lo, hi)))
+            nc.vector.tensor_tensor(low[:], a[:], b[:], ALU.min)
+            for t in range(1, PACK):
+                nc.vector.tensor_copy(c[:, t, :], d[t][:].indirect(entries(n3_t, lo, hi)))
+            nc.vector.tensor_tensor(top[:], low[:], c[:], ALU.max)
+            z_in[i] = sb(f"z_in{i}", [P, n, PACK], BF16)
+            for t in range(PACK):
+                nc.scalar.activation(z_in[i][:, :, t], top[:, t, :], COPY, scale=gs_t[:, t : t + 1])
+
+        def coded_layer(i, banks):
+            lo, hi = PIECES[i]
+            n = hi - lo
+            codes = sb(f"z_codes{i}", [P, n], U32)
+            plane = sb(f"z_plane{i}", [P, n], U8)
+            nc.vector.quantize_mx(out=codes[:].bitcast(FP8X4), scales=plane[:], in_=z_in[i][:].rearrange("p n t -> p (n t)"))
+            for t in ORDER:
+                nc.tensor.matmul_mx(
+                    out=banks[t][:, lo:hi],
+                    lhsT=dk_codes[:, P * t : P * (t + 1)].bitcast(FP8X4),
+                    lhsT_scale=dk_plane[:, P * t : P * (t + 1)],
+                    rhs=codes[:].bitcast(FP8X4),
+                    rhs_scale=plane[:],
+                    start=True, stop=True,
+                )
+
+        def leave_psum(banks, lo, hi):
+            for t in ORDER[:-1]:
+                nc.scalar.activation(h[t][:, lo:hi], banks[t][:, lo:hi], COPY, scale=0.0625)
+
+        def put(t, lo, hi):
+            nc.vector.tensor_copy(page[t][:].indirect(entries(n4_t, lo, hi)), h[t][:, lo:hi])
+
+        upper_part(0, *lower_part(0))
+        ab = lower_part(1)
+        upper_part(1, *ab)
+        coded_layer(0, early)
+        ab = lower_part(2)
+        coded_layer(1, early)
+        leave_psum(early, PIECES[0][0], PIECES[1][1])
+        upper_part(2, *ab)
+        put(FIRST, *PIECES[0])
+        coded_layer(2, late)
+        leave_psum(late, *PIECES[2])
+        put(FIRST, *PIECES[1])
+        put(FIRST, *PIECES[2])
+
+        out_rows = out_0.rearrange("(p t) w -> p t w", t=PACK)
+        grouped = [sb(f"grouped{u}", [P, HALF, PACK], BF16) for u in range(2)]
+        for t in ORDER:
+            if t != FIRST:
+                put(t, 0, S)
+            nc.sync.dma_start(out_rows[:, t, :], page[t][:])
+            for u in range(2):
+                src = page[t][:, u * HALF : (u + 1) * HALF]
+                if t == LAST and u == 0:
+                    nc.vector.tensor_copy(grouped[u][:, :, t], src)
+                else:
+                    nc.scalar.copy(grouped[u][:, :, t], src)
+                if t == FIRST and u == 0:
+                    h[LAST] = keep.tile([P, S], F32, name="h_last", tag=f"h{FIRST}", align_bytes=64)
+                    nc.scalar.activation(h[LAST][:], early[LAST][:], COPY, scale=0.0625)
+
+        out_words = out_1[0].rearrange("p c r -> p (c r)").bitcast(I32)
+        out_plane = sb("out_plane", [P, U], U8)
+        for u in range(2):
+            codes = sb(f"out_codes{u}", [P, HALF], U32)
+            nc.vector.quantize_mx(
+                out=codes[:].bitcast(FP8X4), scales=out_plane[:, u * HALF : (u + 1) * HALF],
+                in_=grouped[u][:].rearrange("p n t -> p (n t)"))
+            nc.sync.dma_start(out_words[:, u * HALF : (u + 1) * HALF], codes[:].bitcast(I32))
+        plane_rows = out_2[0].bitcast(I32)
+        for q in range(4):
+            queue = nc.scalar if q % 2 else nc.sync
+            queue.dma_start(plane_rows[4 * q : 4 * q + 4, :], out_plane[32 * q : 32 * q + 4, :].bitcast(I32))

@@ -14,12 +14,13 @@ U8 = mybir.dt.uint8
 FP8X4 = mybir.dt.float8_e4m3fn_x4
 FP4X4 = mybir.dt.float4_e2m1fn_x4
 ALU = mybir.AluOpType
-COPY = mybir.ActivationFunctionType.Copy
+ACT = mybir.ActivationFunctionType
+COPY = ACT.Copy
 
 P = 128
 PACK = 4
 PIECES = ((0, 256), (256, 384), (384, 512))
-HALF = U // 2
+SPLIT = 768
 FIRST, LAST = 2, 3
 ORDER = (FIRST, 0, 1, LAST)
 
@@ -33,8 +34,8 @@ def tile_picked_twqclampbpage_none_po_kernel(
         keep = ctx.enter_context(tc.tile_pool(name="keep", bufs=1))
         psum = ctx.enter_context(tc.psum_pool(name="psum", bufs=1))
 
-        def sb(name, shape, dtype):
-            return keep.tile(shape, dtype, name=name, align_bytes=64)
+        def sb(name, shape, dtype, tag=None):
+            return keep.tile(shape, dtype, name=name, tag=tag or name, align_bytes=64)
 
         def load_list(name, src):
             tile = keep.tile([P, S // 16], U16, name=name)
@@ -60,35 +61,34 @@ def tile_picked_twqclampbpage_none_po_kernel(
         ds = zeroed_bytes("ds", G)
         dk_plane = zeroed_bytes("dk_plane", H)
 
+        gs_t = sb("gs_t", [P, PACK], F32)
+        nc.gpsimd.dma_start(gs_t[:], gs.rearrange("(p t) o -> p (t o)", t=PACK))
         w1w = sb("w1w", [P, 2 * H], U8)
         nc.sync.dma_start(w1w[:].bitcast(I32), w1_words[0].bitcast(I32))
         offs_t = load_list("offs_t", offs)
         xw = sb("xw", [P, T], U32)
         nc.sync.dma_start(xw[:].bitcast(I32), x_words[0].rearrange("p c r -> p (c r)").bitcast(I32))
         load_plane(xs, x_scales)
+        load_plane(w1s, w1_scales)
+        two_t = load_list("two_t", two)
         w2w = sb("w2w", [P, 2 * H], U8)
         nc.sync.dma_start(w2w[:].bitcast(I32), w2_words[0].bitcast(I32))
-        two_t = load_list("two_t", two)
-        load_plane(w1s, w1_scales)
         load_plane(w2s, w2_scales)
+        n1_t = load_list("n1_t", n1)
         k1_t = load_list("k1_t", k1)
         dw = sb("dw", [P, G], U32)
         nc.sync.dma_start(dw[:].bitcast(I32), d_words[0].rearrange("p c r -> p (c r)").bitcast(I32))
         d_rows = d_scales[0].bitcast(I32)
         for e in range(2):
             nc.sync.dma_start(ds[e:P:16, :].bitcast(I32), d_rows[e:16:2, :])
-        n1_t = load_list("n1_t", n1)
         n2_t = load_list("n2_t", n2)
         n3_t = load_list("n3_t", n3)
-        gs_t = sb("gs_t", [P, PACK], F32)
-        nc.sync.dma_start(gs_t[:], gs.rearrange("(p t) o -> p (t o)", t=PACK))
         n4_t = load_list("n4_t", n4)
         mem_rows = mem.rearrange("(p t) w -> p t w", t=PACK)
-        page = []
-        for t in range(PACK):
-            tile = sb(f"page{t}", [P, U], F32)
-            nc.sync.dma_start(tile[:], mem_rows[:, t, :])
-            page.append(tile)
+        page = {}
+        for t in ORDER:
+            page[t] = sb(f"page{t}", [P, U], F32)
+            nc.sync.dma_start(page[t][:], mem_rows[:, t, :])
 
         def deal(name, src, dtype, per_column):
             dst = sb(name, [P, H * per_column], dtype)
@@ -106,10 +106,7 @@ def tile_picked_twqclampbpage_none_po_kernel(
             nc.vector.tensor_copy(dst[:], table[:].indirect(lst[:]))
             return dst
 
-        def project(tag, w_codes, w_plane, lst):
-            w_dealt = deal(tag + "_wd", w_codes, U8, 2)
-            codes = pick(tag + "_xw", xw, lst, U32)
-            plane = pick(tag + "_xs", xs, lst, U8)
+        def project(tag, w_dealt, w_plane, codes, plane):
             s_dealt = deal(tag + "_sd", w_plane, U8, 1)
             banks = []
             for t in range(PACK):
@@ -125,54 +122,67 @@ def tile_picked_twqclampbpage_none_po_kernel(
                 banks.append(bank)
             return banks
 
+        w1_dealt = deal("w1_dealt", w1w, U8, 2)
+        gs_size = sb("gs_size", [P, PACK], F32)
+        gs_half = sb("gs_half", [P, PACK], F32)
+        gs_sign = sb("gs_sign", [P, PACK], F32)
+        nc.scalar.activation(gs_size[:], gs_t[:], ACT.Abs)
+        nc.scalar.activation(gs_half[:], gs_size[:], COPY, scale=-0.5)
+        nc.scalar.activation(gs_sign[:], gs_t[:], ACT.Sign)
+
         y, y_half, d = [], [], []
-        for t, bank in enumerate(project("y", w1w, w1s, offs_t)):
+        for t, bank in enumerate(project("y", w1_dealt, w1s, pick("y_xw", xw, offs_t, U32), pick("y_xs", xs, offs_t, U8))):
             y_half.append(sb(f"y_half{t}", [P, S], F32))
-            nc.scalar.activation(y_half[t][:], bank[:], COPY, scale=-0.5)
+            nc.scalar.activation(y_half[t][:], bank[:], COPY, scale=gs_half[:, t : t + 1])
             y.append(sb(f"y{t}", [P, S], F32))
-            nc.scalar.copy(y[t][:], bank[:])
-        for t, bank in enumerate(project("d", w2w, w2s, two_t)):
+            nc.scalar.activation(y[t][:], bank[:], COPY, scale=gs_size[:, t : t + 1])
+        two_picked = pick("d_xw", xw, two_t, U32), pick("d_xs", xs, two_t, U8)
+        w2_dealt = deal("w2_dealt", w2w, U8, 2)
+        for t, bank in enumerate(project("d", w2_dealt, w2s, *two_picked)):
             d.append(sb(f"d{t}", [P, S], F32))
-            nc.scalar.copy(d[t][:], bank[:])
+            nc.scalar.activation(d[t][:], bank[:], COPY, scale=gs_size[:, t : t + 1])
 
-        dk_bytes = pick("dk_bytes", ds, k1_t, U8)
-        dk_words = pick("dk_words", dw, k1_t, U32)
-        dk_bytes_dealt = deal("dk_bytes_dealt", dk_bytes, U8, 1)
-        dk_codes = deal("dk_codes", dk_words, U32, 1)
-        for r in range(4):
-            first = 16 * (r // 2) + r % 2
-            nc.sync.dma_start(dk_plane[r:P:32, :].bitcast(I32), dk_bytes_dealt[first:P:32, :].bitcast(I32))
-
-        h = {t: keep.tile([P, S], F32, name=f"h{t}", tag=f"h{t}", align_bytes=64) for t in ORDER[:-1]}
-        early = [psum.tile([P, S], F32, name=f"early{t}", tag=f"y{t}") for t in range(PACK)]
-        late = [psum.tile([P, S], F32, name=f"late{t}", tag=f"d{t}") for t in range(PACK - 1)] + [early[LAST]]
+        banks = [psum.tile([P, S], F32, name=f"h_bank{t}", tag=f"y{t}") for t in range(PACK)]
+        spare_bank = psum.tile([P, S], F32, name="h_spare_bank", tag="d0")
         z_in = {}
+        a_f32 = sb("a_f32", [P, PACK, S], F32)
+        a = [sb(f"a{u}", [P, PACK, S // 2], BF16) for u in range(2)]
+        low = [sb(f"low{u}", [P, PACK, S // 2], BF16) for u in range(2)]
 
-        def lower_part(i):
-            lo, hi = PIECES[i]
-            n = hi - lo
-            a = sb(f"a{i}", [P, PACK, n], F32)
-            b = sb(f"b{i}", [P, PACK, n], F32)
+        def own_stream(u):
+            lo, hi = u * S // 2, (u + 1) * S // 2
             for t in range(PACK):
-                nc.vector.tensor_tensor(a[:, t, :], y_half[t][:].indirect(entries(n1_t, lo, hi)), y[t][:, lo:hi], ALU.add)
+                nc.vector.tensor_tensor(
+                    a_f32[:, t, lo:hi], y_half[t][:].indirect(entries(n1_t, lo, hi)), y[t][:, lo:hi], ALU.add)
+            nc.scalar.copy(a[u][:], a_f32[:, :, lo:hi])
+
+        def lower_bound(u):
+            lo, hi = u * S // 2, (u + 1) * S // 2
+            b = sb(f"b{u}", [P, PACK, S // 2], BF16)
             for t in range(PACK):
                 nc.vector.tensor_copy(b[:, t, :], d[t][:].indirect(entries(n2_t, lo, hi)))
-            return a, b
+            return b
 
-        def upper_part(i, a, b):
+        def upper_part(i, b=None):
             lo, hi = PIECES[i]
             n = hi - lo
-            low = sb(f"low{i}", [P, PACK, n], F32)
-            c = sb(f"c{i}", [P, PACK, n], F32)
-            top = sb(f"top{i}", [P, PACK, n], F32)
-            nc.vector.tensor_copy(c[:, 0, :], d[0][:].indirect(entries(n3_t, lo, hi)))
-            nc.vector.tensor_tensor(low[:], a[:], b[:], ALU.min)
-            for t in range(1, PACK):
-                nc.vector.tensor_copy(c[:, t, :], d[t][:].indirect(entries(n3_t, lo, hi)))
-            nc.vector.tensor_tensor(top[:], low[:], c[:], ALU.max)
+            u, at = divmod(lo, S // 2)
+            picked = sb(f"c{i}", [P, PACK, n], BF16)
+            c = [picked[:, t, :] for t in range(PACK)]
+            top = sb(f"top{i}", [P, PACK, n], BF16)
             z_in[i] = sb(f"z_in{i}", [P, n, PACK], BF16)
-            for t in range(PACK):
-                nc.scalar.activation(z_in[i][:, :, t], top[:, t, :], COPY, scale=gs_t[:, t : t + 1])
+
+            def finish(t):
+                nc.vector.tensor_tensor(top[:, t, :], low[u][:, t, at : at + n], c[t], ALU.max)
+                nc.scalar.activation(z_in[i][:, :, t], top[:, t, :], COPY, scale=gs_sign[:, t : t + 1])
+
+            nc.vector.tensor_copy(c[0], d[0][:].indirect(entries(n3_t, lo, hi)))
+            if b is not None:
+                nc.vector.tensor_tensor(low[u][:], a[u][:], b[:], ALU.min)
+            for t in range(1, PACK):
+                nc.vector.tensor_copy(c[t], d[t][:].indirect(entries(n3_t, lo, hi)))
+                finish(t - 1)
+            finish(PACK - 1)
 
         def coded_layer(i, banks):
             lo, hi = PIECES[i]
@@ -190,51 +200,62 @@ def tile_picked_twqclampbpage_none_po_kernel(
                     start=True, stop=True,
                 )
 
-        def leave_psum(banks, lo, hi):
-            for t in ORDER[:-1]:
-                nc.scalar.activation(h[t][:, lo:hi], banks[t][:, lo:hi], COPY, scale=0.0625)
+        def leave_psum(name, bank, lo, hi, tag=None):
+            tile = sb(name, [P, hi - lo], F32, tag=tag)
+            nc.scalar.activation(tile[:], bank[:, lo:hi], COPY, scale=0.0625)
+            return tile
 
-        def put(t, lo, hi):
-            nc.vector.tensor_copy(page[t][:].indirect(entries(n4_t, lo, hi)), h[t][:, lo:hi])
+        def put(t, values, lo, hi):
+            nc.vector.tensor_copy(page[t][:].indirect(entries(n4_t, lo, hi)), values[:])
 
-        upper_part(0, *lower_part(0))
-        ab = lower_part(1)
-        upper_part(1, *ab)
-        coded_layer(0, early)
-        ab = lower_part(2)
-        coded_layer(1, early)
-        leave_psum(early, PIECES[0][0], PIECES[1][1])
-        upper_part(2, *ab)
-        put(FIRST, *PIECES[0])
-        coded_layer(2, late)
-        leave_psum(late, *PIECES[2])
-        put(FIRST, *PIECES[1])
-        put(FIRST, *PIECES[2])
+        own_stream(0)
+        own_stream(1)
+        dk_bytes = pick("dk_bytes", ds, k1_t, U8)
+        dk_words = pick("dk_words", dw, k1_t, U32)
+        dk_bytes_dealt = deal("dk_bytes_dealt", dk_bytes, U8, 1)
+        dk_codes = deal("dk_codes", dk_words, U32, 1)
+        for r in range(4):
+            first = 16 * (r // 2) + r % 2
+            nc.sync.dma_start(dk_plane[r:P:32, :].bitcast(I32), dk_bytes_dealt[first:P:32, :].bitcast(I32))
+
+        upper_part(0, lower_bound(0))
+        b = lower_bound(1)
+        coded_layer(0, banks)
+        upper_part(1, b)
+        coded_layer(1, banks)
+        h_early = leave_psum("h_early", banks[FIRST], 0, PIECES[2][0])
+        upper_part(2)
+        coded_layer(2, [spare_bank if t == FIRST else banks[t] for t in range(PACK)])
+        put(FIRST, h_early, 0, PIECES[2][0])
+        put(FIRST, leave_psum("h_late", spare_bank, *PIECES[2]), *PIECES[2])
+        h = {t: leave_psum(f"h{t}", banks[t], 0, S) for t in ORDER[1:-1]}
 
         out_rows = out_0.rearrange("(p t) w -> p t w", t=PACK)
-        grouped = [sb(f"grouped{u}", [P, HALF, PACK], BF16) for u in range(2)]
+        spans = ((0, SPLIT), (SPLIT, U))
+        grouped = [sb(f"grouped{u}", [P, hi - lo, PACK], BF16) for u, (lo, hi) in enumerate(spans)]
         for t in ORDER:
             if t != FIRST:
-                put(t, 0, S)
+                put(t, h[t], 0, S)
             nc.sync.dma_start(out_rows[:, t, :], page[t][:])
-            for u in range(2):
-                src = page[t][:, u * HALF : (u + 1) * HALF]
-                if t == LAST and u == 0:
-                    nc.vector.tensor_copy(grouped[u][:, :, t], src)
-                else:
-                    nc.scalar.copy(grouped[u][:, :, t], src)
-                if t == FIRST and u == 0:
-                    h[LAST] = keep.tile([P, S], F32, name="h_last", tag=f"h{FIRST}", align_bytes=64)
-                    nc.scalar.activation(h[LAST][:], early[LAST][:], COPY, scale=0.0625)
+            if t == LAST:
+                nc.scalar.copy(grouped[1][:, :, t], page[t][:, SPLIT:U])
+                for lo, hi in ((0, 512), (512, SPLIT)):
+                    nc.vector.tensor_copy(grouped[0][:, lo:hi, t], page[t][:, lo:hi])
+            else:
+                nc.scalar.copy(grouped[0][:, :, t], page[t][:, 0:SPLIT])
+                if t == FIRST:
+                    h[LAST] = leave_psum("h_last", banks[LAST], 0, S, tag="h_late")
+                nc.scalar.copy(grouped[1][:, :, t], page[t][:, SPLIT:U])
 
         out_words = out_1[0].rearrange("p c r -> p (c r)").bitcast(I32)
         out_plane = sb("out_plane", [P, U], U8)
-        for u in range(2):
-            codes = sb(f"out_codes{u}", [P, HALF], U32)
+        for u, lo, hi in ((0, 0, 512), (0, 512, SPLIT), (1, SPLIT, U)):
+            codes = sb(f"out_codes{lo}", [P, hi - lo], U32)
+            base = spans[u][0]
             nc.vector.quantize_mx(
-                out=codes[:].bitcast(FP8X4), scales=out_plane[:, u * HALF : (u + 1) * HALF],
-                in_=grouped[u][:].rearrange("p n t -> p (n t)"))
-            nc.sync.dma_start(out_words[:, u * HALF : (u + 1) * HALF], codes[:].bitcast(I32))
+                out=codes[:].bitcast(FP8X4), scales=out_plane[:, lo:hi],
+                in_=grouped[u][:, lo - base : hi - base, :].rearrange("p n t -> p (n t)"))
+            nc.sync.dma_start(out_words[:, lo:hi], codes[:].bitcast(I32))
         plane_rows = out_2[0].bitcast(I32)
         for q in range(4):
             queue = nc.scalar if q % 2 else nc.sync

@@ -3,7 +3,7 @@ from contextlib import ExitStack
 import concourse.mybir as mybir
 
 K, T, S, H, G, U = 512, 1024, 512, 512, 2048, 1024
-FLOPS = 3 * 2 * 512 * 512 * 512
+FLOPS = 3 * 2 * K * H * S
 
 F32 = mybir.dt.float32
 BF16 = mybir.dt.bfloat16
@@ -15,14 +15,16 @@ FP8X4 = mybir.dt.float8_e4m3fn_x4
 FP4X4 = mybir.dt.float4_e2m1fn_x4
 ALU = mybir.AluOpType
 ACT = mybir.ActivationFunctionType
-COPY = ACT.Copy
 
 P = 128
 PACK = 4
+QUADRANTS = 4
+HALF = S // 2
 PIECES = ((0, 256), (256, 384), (384, 512))
-SPLIT = 768
 FIRST, LAST = 2, 3
 ORDER = (FIRST, 0, 1, LAST)
+SPLIT = 768
+QUANT_CUT = 512
 
 
 def tile_picked_twqclampbpage_none_po_kernel(
@@ -49,7 +51,7 @@ def tile_picked_twqclampbpage_none_po_kernel(
 
         def load_plane(tile, src):
             rows = src[0].bitcast(I32)
-            for q in range(4):
+            for q in range(QUADRANTS):
                 nc.sync.dma_start(tile[32 * q : 32 * q + 4, :].bitcast(I32), rows[4 * q : 4 * q + 4, :])
 
         def entries(lst, lo, hi):
@@ -107,109 +109,107 @@ def tile_picked_twqclampbpage_none_po_kernel(
             return dst
 
         def project(tag, w_dealt, w_plane, codes, plane):
-            s_dealt = deal(tag + "_sd", w_plane, U8, 1)
-            banks = []
+            plane_dealt = deal(tag + "_plane_dealt", w_plane, U8, 1)
+            result = []
             for t in range(PACK):
                 bank = psum.tile([P, S], F32, name=f"{tag}_bank{t}", tag=f"{tag}{t}")
                 nc.tensor.matmul_mx(
                     out=bank[:],
                     lhsT=w_dealt[:, 2 * P * t : 2 * P * (t + 1)].bitcast(FP4X4),
-                    lhsT_scale=s_dealt[:, P * t : P * (t + 1)],
+                    lhsT_scale=plane_dealt[:, P * t : P * (t + 1)],
                     rhs=codes[:].bitcast(FP8X4),
                     rhs_scale=plane[:],
                     start=True, stop=True,
                 )
-                banks.append(bank)
-            return banks
+                result.append(bank)
+            return result
 
         w1_dealt = deal("w1_dealt", w1w, U8, 2)
         gs_size = sb("gs_size", [P, PACK], F32)
         gs_half = sb("gs_half", [P, PACK], F32)
         gs_sign = sb("gs_sign", [P, PACK], F32)
         nc.scalar.activation(gs_size[:], gs_t[:], ACT.Abs)
-        nc.scalar.activation(gs_half[:], gs_size[:], COPY, scale=-0.5)
+        nc.scalar.activation(gs_half[:], gs_size[:], ACT.Copy, scale=-0.5)
         nc.scalar.activation(gs_sign[:], gs_t[:], ACT.Sign)
 
-        y, y_half, d = [], [], []
-        for t, bank in enumerate(project("y", w1_dealt, w1s, pick("y_xw", xw, offs_t, U32), pick("y_xs", xs, offs_t, U8))):
-            y_half.append(sb(f"y_half{t}", [P, S], F32))
-            nc.scalar.activation(y_half[t][:], bank[:], COPY, scale=gs_half[:, t : t + 1])
-            y.append(sb(f"y{t}", [P, S], F32))
-            nc.scalar.activation(y[t][:], bank[:], COPY, scale=gs_size[:, t : t + 1])
+        y_window = [sb(f"y_window{t}", [P, 2 * S], F32) for t in range(PACK)]
+        y = [y_window[(t + 1) % PACK][:, S:] for t in range(PACK)]
+        offs_picked = pick("y_xw", xw, offs_t, U32), pick("y_xs", xs, offs_t, U8)
+        for t, bank in enumerate(project("y", w1_dealt, w1s, *offs_picked)):
+            nc.scalar.activation(y_window[t][:, :S], bank[:], ACT.Copy, scale=gs_half[:, t : t + 1])
+            nc.scalar.activation(y[t], bank[:], ACT.Copy, scale=gs_size[:, t : t + 1])
         two_picked = pick("d_xw", xw, two_t, U32), pick("d_xs", xs, two_t, U8)
         w2_dealt = deal("w2_dealt", w2w, U8, 2)
+        d = []
         for t, bank in enumerate(project("d", w2_dealt, w2s, *two_picked)):
             d.append(sb(f"d{t}", [P, S], F32))
-            nc.scalar.activation(d[t][:], bank[:], COPY, scale=gs_size[:, t : t + 1])
+            nc.scalar.activation(d[t][:], bank[:], ACT.Copy, scale=gs_size[:, t : t + 1])
 
-        banks = [psum.tile([P, S], F32, name=f"h_bank{t}", tag=f"y{t}") for t in range(PACK)]
+        h_banks = [psum.tile([P, S], F32, name=f"h_bank{t}", tag=f"y{t}") for t in range(PACK)]
         spare_bank = psum.tile([P, S], F32, name="h_spare_bank", tag="d0")
         z_in = {}
-        a_f32 = sb("a_f32", [P, PACK, S], F32)
-        a = [sb(f"a{u}", [P, PACK, S // 2], BF16) for u in range(2)]
-        low = [sb(f"low{u}", [P, PACK, S // 2], BF16) for u in range(2)]
+        own_f32 = sb("own_f32", [P, PACK, S], F32)
+        own = [sb(f"own{u}", [P, PACK, HALF], BF16) for u in range(2)]
+        low = [sb(f"low{u}", [P, PACK, HALF], BF16) for u in range(2)]
 
-        def own_stream(u):
-            lo, hi = u * S // 2, (u + 1) * S // 2
+        n2_buffers = ("by_n2_0", "by_n3_0")
+        n3_buffers = ("by_n3_0", "by_n2_0", "own0")
+
+        def pick_n2(u):
+            picked = sb(f"by_n2_{u}", [P, PACK, HALF], BF16, tag=n2_buffers[u])
             for t in range(PACK):
-                nc.vector.tensor_tensor(
-                    a_f32[:, t, lo:hi], y_half[t][:].indirect(entries(n1_t, lo, hi)), y[t][:, lo:hi], ALU.add)
-            nc.scalar.copy(a[u][:], a_f32[:, :, lo:hi])
+                nc.vector.tensor_copy(picked[:, t, :], d[t][:].indirect(entries(n2_t, u * HALF, (u + 1) * HALF)))
+            return picked
 
-        def lower_bound(u):
-            lo, hi = u * S // 2, (u + 1) * S // 2
-            b = sb(f"b{u}", [P, PACK, S // 2], BF16)
-            for t in range(PACK):
-                nc.vector.tensor_copy(b[:, t, :], d[t][:].indirect(entries(n2_t, lo, hi)))
-            return b
-
-        def upper_part(i, b=None):
+        def clamp(i, by_n2=None):
             lo, hi = PIECES[i]
             n = hi - lo
-            u, at = divmod(lo, S // 2)
-            picked = sb(f"c{i}", [P, PACK, n], BF16)
-            c = [picked[:, t, :] for t in range(PACK)]
+            u, at = divmod(lo, HALF)
+            by_n3 = sb(f"by_n3_{i}", [P, PACK, n], BF16, tag=n3_buffers[i])
             top = sb(f"top{i}", [P, PACK, n], BF16)
             z_in[i] = sb(f"z_in{i}", [P, n, PACK], BF16)
 
             def finish(t):
-                nc.vector.tensor_tensor(top[:, t, :], low[u][:, t, at : at + n], c[t], ALU.max)
-                nc.scalar.activation(z_in[i][:, :, t], top[:, t, :], COPY, scale=gs_sign[:, t : t + 1])
+                nc.vector.tensor_tensor(top[:, t, :], low[u][:, t, at : at + n], by_n3[:, t, :], ALU.max)
+                nc.scalar.activation(z_in[i][:, :, t], top[:, t, :], ACT.Copy, scale=gs_sign[:, t : t + 1])
 
-            nc.vector.tensor_copy(c[0], d[0][:].indirect(entries(n3_t, lo, hi)))
-            if b is not None:
-                nc.vector.tensor_tensor(low[u][:], a[u][:], b[:], ALU.min)
+            nc.vector.tensor_copy(by_n3[:, 0, :], d[0][:].indirect(entries(n3_t, lo, hi)))
+            if by_n2 is not None:
+                nc.vector.tensor_tensor(low[u][:], own[u][:], by_n2[:], ALU.min)
             for t in range(1, PACK):
-                nc.vector.tensor_copy(c[t], d[t][:].indirect(entries(n3_t, lo, hi)))
+                nc.vector.tensor_copy(by_n3[:, t, :], d[t][:].indirect(entries(n3_t, lo, hi)))
                 finish(t - 1)
             finish(PACK - 1)
 
         def coded_layer(i, banks):
             lo, hi = PIECES[i]
-            n = hi - lo
-            codes = sb(f"z_codes{i}", [P, n], U32)
-            plane = sb(f"z_plane{i}", [P, n], U8)
-            nc.vector.quantize_mx(out=codes[:].bitcast(FP8X4), scales=plane[:], in_=z_in[i][:].rearrange("p n t -> p (n t)"))
+            z_codes = sb(f"z_codes{i}", [P, hi - lo], U32)
+            z_plane = sb(f"z_plane{i}", [P, hi - lo], U8)
+            nc.vector.quantize_mx(
+                out=z_codes[:].bitcast(FP8X4), scales=z_plane[:], in_=z_in[i][:].rearrange("p n t -> p (n t)"))
             for t in ORDER:
                 nc.tensor.matmul_mx(
                     out=banks[t][:, lo:hi],
                     lhsT=dk_codes[:, P * t : P * (t + 1)].bitcast(FP8X4),
                     lhsT_scale=dk_plane[:, P * t : P * (t + 1)],
-                    rhs=codes[:].bitcast(FP8X4),
-                    rhs_scale=plane[:],
+                    rhs=z_codes[:].bitcast(FP8X4),
+                    rhs_scale=z_plane[:],
                     start=True, stop=True,
                 )
 
         def leave_psum(name, bank, lo, hi, tag=None):
             tile = sb(name, [P, hi - lo], F32, tag=tag)
-            nc.scalar.activation(tile[:], bank[:, lo:hi], COPY, scale=0.0625)
+            nc.scalar.activation(tile[:], bank[:, lo:hi], ACT.Copy, scale=0.0625)
             return tile
 
         def put(t, values, lo, hi):
             nc.vector.tensor_copy(page[t][:].indirect(entries(n4_t, lo, hi)), values[:])
 
-        own_stream(0)
-        own_stream(1)
+        for t in (1, 2, 3, 0):
+            nc.vector.tensor_tensor(own_f32[:, t, :], y_window[t][:].indirect(n1_t[:]), y[t], ALU.add)
+        for u in range(2):
+            nc.scalar.copy(own[u][:], own_f32[:, :, u * HALF : (u + 1) * HALF])
+
         dk_bytes = pick("dk_bytes", ds, k1_t, U8)
         dk_words = pick("dk_words", dw, k1_t, U32)
         dk_bytes_dealt = deal("dk_bytes_dealt", dk_bytes, U8, 1)
@@ -218,17 +218,18 @@ def tile_picked_twqclampbpage_none_po_kernel(
             first = 16 * (r // 2) + r % 2
             nc.sync.dma_start(dk_plane[r:P:32, :].bitcast(I32), dk_bytes_dealt[first:P:32, :].bitcast(I32))
 
-        upper_part(0, lower_bound(0))
-        b = lower_bound(1)
-        coded_layer(0, banks)
-        upper_part(1, b)
-        coded_layer(1, banks)
-        h_early = leave_psum("h_early", banks[FIRST], 0, PIECES[2][0])
-        upper_part(2)
-        coded_layer(2, [spare_bank if t == FIRST else banks[t] for t in range(PACK)])
-        put(FIRST, h_early, 0, PIECES[2][0])
-        put(FIRST, leave_psum("h_late", spare_bank, *PIECES[2]), *PIECES[2])
-        h = {t: leave_psum(f"h{t}", banks[t], 0, S) for t in ORDER[1:-1]}
+        clamp(0, pick_n2(0))
+        second_half = pick_n2(1)
+        coded_layer(0, h_banks)
+        h_early = leave_psum("h_early", h_banks[FIRST], 0, HALF)
+        late_banks = [spare_bank if t == FIRST else h_banks[t] for t in range(PACK)]
+        clamp(1, second_half)
+        coded_layer(1, late_banks)
+        clamp(2)
+        coded_layer(2, late_banks)
+        put(FIRST, h_early, 0, HALF)
+        put(FIRST, leave_psum("h_late", spare_bank, HALF, S), HALF, S)
+        h = {t: leave_psum(f"h{t}", h_banks[t], 0, S) for t in ORDER[1:-1]}
 
         out_rows = out_0.rearrange("(p t) w -> p t w", t=PACK)
         spans = ((0, SPLIT), (SPLIT, U))
@@ -239,24 +240,24 @@ def tile_picked_twqclampbpage_none_po_kernel(
             nc.sync.dma_start(out_rows[:, t, :], page[t][:])
             if t == LAST:
                 nc.scalar.copy(grouped[1][:, :, t], page[t][:, SPLIT:U])
-                for lo, hi in ((0, 512), (512, SPLIT)):
+                for lo, hi in ((0, QUANT_CUT), (QUANT_CUT, SPLIT)):
                     nc.vector.tensor_copy(grouped[0][:, lo:hi, t], page[t][:, lo:hi])
             else:
                 nc.scalar.copy(grouped[0][:, :, t], page[t][:, 0:SPLIT])
                 if t == FIRST:
-                    h[LAST] = leave_psum("h_last", banks[LAST], 0, S, tag="h_late")
+                    h[LAST] = leave_psum("h_last", h_banks[LAST], 0, S, tag="h_late")
                 nc.scalar.copy(grouped[1][:, :, t], page[t][:, SPLIT:U])
 
         out_words = out_1[0].rearrange("p c r -> p (c r)").bitcast(I32)
         out_plane = sb("out_plane", [P, U], U8)
-        for u, lo, hi in ((0, 0, 512), (0, 512, SPLIT), (1, SPLIT, U)):
-            codes = sb(f"out_codes{lo}", [P, hi - lo], U32)
+        for u, lo, hi in ((0, 0, QUANT_CUT), (0, QUANT_CUT, SPLIT), (1, SPLIT, U)):
+            out_codes = sb(f"out_codes{lo}", [P, hi - lo], U32)
             base = spans[u][0]
             nc.vector.quantize_mx(
-                out=codes[:].bitcast(FP8X4), scales=out_plane[:, lo:hi],
+                out=out_codes[:].bitcast(FP8X4), scales=out_plane[:, lo:hi],
                 in_=grouped[u][:, lo - base : hi - base, :].rearrange("p n t -> p (n t)"))
-            nc.sync.dma_start(out_words[:, lo:hi], codes[:].bitcast(I32))
+            nc.sync.dma_start(out_words[:, lo:hi], out_codes[:].bitcast(I32))
         plane_rows = out_2[0].bitcast(I32)
-        for q in range(4):
+        for q in range(QUADRANTS):
             queue = nc.scalar if q % 2 else nc.sync
             queue.dma_start(plane_rows[4 * q : 4 * q + 4, :], out_plane[32 * q : 32 * q + 4, :].bitcast(I32))

@@ -152,8 +152,8 @@ def tile_picked_twqclampbpage_none_po_kernel(
         own = [sb(f"own{u}", [P, PACK, HALF], BF16) for u in range(2)]
         low = [sb(f"low{u}", [P, PACK, HALF], BF16) for u in range(2)]
 
-        n2_buffers = ("by_n2_0", "by_n3_0")
-        n3_buffers = ("by_n3_0", "by_n2_0", "own0")
+        n2_buffers = ("by_n2_0", "own0")
+        n3_buffers = ("by_n3_0", "by_n3_0", "own0")
 
         def pick_n2(u):
             picked = sb(f"by_n2_{u}", [P, PACK, HALF], BF16, tag=n2_buffers[u])

from contextlib import ExitStack

import concourse.mybir as mybir

K, T, S, H, G, U = 512, 1024, 512, 512, 2048, 1024
FLOPS = 3 * 2 * K * H * S

F32 = mybir.dt.float32
BF16 = mybir.dt.bfloat16
I32 = mybir.dt.int32
U32 = mybir.dt.uint32
U16 = mybir.dt.uint16
U8 = mybir.dt.uint8
FP8X4 = mybir.dt.float8_e4m3fn_x4
FP4X4 = mybir.dt.float4_e2m1fn_x4
ALU = mybir.AluOpType
ACT = mybir.ActivationFunctionType

P = 128
PACK = 4
QUADRANTS = 4
HALF = S // 2
PIECES = ((0, 256), (256, 384), (384, 512))
FIRST, LAST = 2, 3
ORDER = (FIRST, 0, 1, LAST)
SPLIT = 768
QUANT_CUT = 512


def tile_picked_twqclampbpage_none_po_kernel(
    tc, x_words, x_scales, w1_words, w1_scales, w2_words, w2_scales, gs, d_words, d_scales, mem,
    offs, two, n1, n2, n3, k1, n4, out_0, out_1, out_2,
):
    nc = tc.nc
    with ExitStack() as ctx:
        keep = ctx.enter_context(tc.tile_pool(name="keep", bufs=1))
        psum = ctx.enter_context(tc.psum_pool(name="psum", bufs=1))

        def sb(name, shape, dtype, tag=None):
            return keep.tile(shape, dtype, name=name, tag=tag or name, align_bytes=64)

        def load_list(name, src):
            tile = keep.tile([P, S // 16], U16, name=name)
            nc.sync.dma_start(tile[:], src)
            return tile

        def zeroed_bytes(name, width):
            tile = sb(name, [P, width], U8)
            nc.vector.memset(tile[:].bitcast(I32), 0)
            return tile

        def load_plane(tile, src):
            rows = src[0].bitcast(I32)
            for q in range(QUADRANTS):
                nc.sync.dma_start(tile[32 * q : 32 * q + 4, :].bitcast(I32), rows[4 * q : 4 * q + 4, :])

        def entries(lst, lo, hi):
            return lst[:, lo // 16 : hi // 16]

        xs = zeroed_bytes("xs", T)
        w1s = zeroed_bytes("w1s", H)
        w2s = zeroed_bytes("w2s", H)
        ds = zeroed_bytes("ds", G)
        dk_plane = zeroed_bytes("dk_plane", H)

        gs_t = sb("gs_t", [P, PACK], F32)
        nc.gpsimd.dma_start(gs_t[:], gs.rearrange("(p t) o -> p (t o)", t=PACK))
        w1w = sb("w1w", [P, 2 * H], U8)
        nc.sync.dma_start(w1w[:].bitcast(I32), w1_words[0].bitcast(I32))
        offs_t = load_list("offs_t", offs)
        xw = sb("xw", [P, T], U32)
        nc.sync.dma_start(xw[:].bitcast(I32), x_words[0].rearrange("p c r -> p (c r)").bitcast(I32))
        load_plane(xs, x_scales)
        load_plane(w1s, w1_scales)
        two_t = load_list("two_t", two)
        w2w = sb("w2w", [P, 2 * H], U8)
        nc.sync.dma_start(w2w[:].bitcast(I32), w2_words[0].bitcast(I32))
        load_plane(w2s, w2_scales)
        n1_t = load_list("n1_t", n1)
        k1_t = load_list("k1_t", k1)
        dw = sb("dw", [P, G], U32)
        nc.sync.dma_start(dw[:].bitcast(I32), d_words[0].rearrange("p c r -> p (c r)").bitcast(I32))
        d_rows = d_scales[0].bitcast(I32)
        for e in range(2):
            nc.sync.dma_start(ds[e:P:16, :].bitcast(I32), d_rows[e:16:2, :])
        n2_t = load_list("n2_t", n2)
        n3_t = load_list("n3_t", n3)
        n4_t = load_list("n4_t", n4)
        mem_rows = mem.rearrange("(p t) w -> p t w", t=PACK)
        page = {}
        for t in ORDER:
            page[t] = sb(f"page{t}", [P, U], F32)
            nc.sync.dma_start(page[t][:], mem_rows[:, t, :])

        def deal(name, src, dtype, per_column):
            dst = sb(name, [P, H * per_column], dtype)
            if per_column == 1:
                nc.vector.tensor_copy(
                    dst[:].rearrange("p (t m) -> p m t", t=PACK), src[:].rearrange("p (m t) -> p m t", t=PACK))
            else:
                nc.vector.tensor_copy(
                    dst[:].rearrange("p (t m b) -> p m t b", t=PACK, b=per_column),
                    src[:].rearrange("p (m t b) -> p m t b", t=PACK, b=per_column))
            return dst

        def pick(name, table, lst, dtype):
            dst = sb(name, [P, S], dtype)
            nc.vector.tensor_copy(dst[:], table[:].indirect(lst[:]))
            return dst

        def project(tag, w_dealt, w_plane, codes, plane):
            plane_dealt = deal(tag + "_plane_dealt", w_plane, U8, 1)
            result = []
            for t in range(PACK):
                bank = psum.tile([P, S], F32, name=f"{tag}_bank{t}", tag=f"{tag}{t}")
                nc.tensor.matmul_mx(
                    out=bank[:],
                    lhsT=w_dealt[:, 2 * P * t : 2 * P * (t + 1)].bitcast(FP4X4),
                    lhsT_scale=plane_dealt[:, P * t : P * (t + 1)],
                    rhs=codes[:].bitcast(FP8X4),
                    rhs_scale=plane[:],
                    start=True, stop=True,
                )
                result.append(bank)
            return result

        w1_dealt = deal("w1_dealt", w1w, U8, 2)
        gs_size = sb("gs_size", [P, PACK], F32)
        gs_half = sb("gs_half", [P, PACK], F32)
        gs_sign = sb("gs_sign", [P, PACK], F32)
        nc.scalar.activation(gs_size[:], gs_t[:], ACT.Abs)
        nc.scalar.activation(gs_half[:], gs_size[:], ACT.Copy, scale=-0.5)
        nc.scalar.activation(gs_sign[:], gs_t[:], ACT.Sign)

        y_window = [sb(f"y_window{t}", [P, 2 * S], F32) for t in range(PACK)]
        y = [y_window[(t + 1) % PACK][:, S:] for t in range(PACK)]
        offs_picked = pick("y_xw", xw, offs_t, U32), pick("y_xs", xs, offs_t, U8)
        for t, bank in enumerate(project("y", w1_dealt, w1s, *offs_picked)):
            nc.scalar.activation(y_window[t][:, :S], bank[:], ACT.Copy, scale=gs_half[:, t : t + 1])
            nc.scalar.activation(y[t], bank[:], ACT.Copy, scale=gs_size[:, t : t + 1])
        two_picked = pick("d_xw", xw, two_t, U32), pick("d_xs", xs, two_t, U8)
        w2_dealt = deal("w2_dealt", w2w, U8, 2)
        d = []
        for t, bank in enumerate(project("d", w2_dealt, w2s, *two_picked)):
            d.append(sb(f"d{t}", [P, S], F32))
            nc.scalar.activation(d[t][:], bank[:], ACT.Copy, scale=gs_size[:, t : t + 1])

        h_banks = [psum.tile([P, S], F32, name=f"h_bank{t}", tag=f"y{t}") for t in range(PACK)]
        spare_bank = psum.tile([P, S], F32, name="h_spare_bank", tag="d0")
        z_in = {}
        own_f32 = sb("own_f32", [P, PACK, S], F32)
        own = [sb(f"own{u}", [P, PACK, HALF], BF16) for u in range(2)]
        low = [sb(f"low{u}", [P, PACK, HALF], BF16) for u in range(2)]

        n2_buffers = ("by_n2_0", "own0")
        n3_buffers = ("by_n3_0", "by_n3_0", "own0")

        def pick_n2(u):
            picked = sb(f"by_n2_{u}", [P, PACK, HALF], BF16, tag=n2_buffers[u])
            for t in range(PACK):
                nc.vector.tensor_copy(picked[:, t, :], d[t][:].indirect(entries(n2_t, u * HALF, (u + 1) * HALF)))
            return picked

        def clamp(i, by_n2=None):
            lo, hi = PIECES[i]
            n = hi - lo
            u, at = divmod(lo, HALF)
            by_n3 = sb(f"by_n3_{i}", [P, PACK, n], BF16, tag=n3_buffers[i])
            top = sb(f"top{i}", [P, PACK, n], BF16)
            z_in[i] = sb(f"z_in{i}", [P, n, PACK], BF16)

            def finish(t):
                nc.vector.tensor_tensor(top[:, t, :], low[u][:, t, at : at + n], by_n3[:, t, :], ALU.max)
                nc.scalar.activation(z_in[i][:, :, t], top[:, t, :], ACT.Copy, scale=gs_sign[:, t : t + 1])

            nc.vector.tensor_copy(by_n3[:, 0, :], d[0][:].indirect(entries(n3_t, lo, hi)))
            if by_n2 is not None:
                nc.vector.tensor_tensor(low[u][:], own[u][:], by_n2[:], ALU.min)
            for t in range(1, PACK):
                nc.vector.tensor_copy(by_n3[:, t, :], d[t][:].indirect(entries(n3_t, lo, hi)))
                finish(t - 1)
            finish(PACK - 1)

        def coded_layer(i, banks):
            lo, hi = PIECES[i]
            z_codes = sb(f"z_codes{i}", [P, hi - lo], U32)
            z_plane = sb(f"z_plane{i}", [P, hi - lo], U8)
            nc.vector.quantize_mx(
                out=z_codes[:].bitcast(FP8X4), scales=z_plane[:], in_=z_in[i][:].rearrange("p n t -> p (n t)"))
            for t in ORDER:
                nc.tensor.matmul_mx(
                    out=banks[t][:, lo:hi],
                    lhsT=dk_codes[:, P * t : P * (t + 1)].bitcast(FP8X4),
                    lhsT_scale=dk_plane[:, P * t : P * (t + 1)],
                    rhs=z_codes[:].bitcast(FP8X4),
                    rhs_scale=z_plane[:],
                    start=True, stop=True,
                )

        def leave_psum(name, bank, lo, hi, tag=None):
            tile = sb(name, [P, hi - lo], F32, tag=tag)
            nc.scalar.activation(tile[:], bank[:, lo:hi], ACT.Copy, scale=0.0625)
            return tile

        def put(t, values, lo, hi):
            nc.vector.tensor_copy(page[t][:].indirect(entries(n4_t, lo, hi)), values[:])

        for t in (1, 2, 3, 0):
            nc.vector.tensor_tensor(own_f32[:, t, :], y_window[t][:].indirect(n1_t[:]), y[t], ALU.add)
        for u in range(2):
            nc.scalar.copy(own[u][:], own_f32[:, :, u * HALF : (u + 1) * HALF])

        dk_bytes = pick("dk_bytes", ds, k1_t, U8)
        dk_words = pick("dk_words", dw, k1_t, U32)
        dk_bytes_dealt = deal("dk_bytes_dealt", dk_bytes, U8, 1)
        dk_codes = deal("dk_codes", dk_words, U32, 1)
        for r in range(4):
            first = 16 * (r // 2) + r % 2
            nc.sync.dma_start(dk_plane[r:P:32, :].bitcast(I32), dk_bytes_dealt[first:P:32, :].bitcast(I32))

        clamp(0, pick_n2(0))
        second_half = pick_n2(1)
        coded_layer(0, h_banks)
        h_early = leave_psum("h_early", h_banks[FIRST], 0, HALF)
        late_banks = [spare_bank if t == FIRST else h_banks[t] for t in range(PACK)]
        clamp(1, second_half)
        coded_layer(1, late_banks)
        clamp(2)
        coded_layer(2, late_banks)
        put(FIRST, h_early, 0, HALF)
        put(FIRST, leave_psum("h_late", spare_bank, HALF, S), HALF, S)
        h = {t: leave_psum(f"h{t}", h_banks[t], 0, S) for t in ORDER[1:-1]}

        out_rows = out_0.rearrange("(p t) w -> p t w", t=PACK)
        spans = ((0, SPLIT), (SPLIT, U))
        grouped = [sb(f"grouped{u}", [P, hi - lo, PACK], BF16) for u, (lo, hi) in enumerate(spans)]
        for t in ORDER:
            if t != FIRST:
                put(t, h[t], 0, S)
            nc.sync.dma_start(out_rows[:, t, :], page[t][:])
            if t == LAST:
                nc.scalar.copy(grouped[1][:, :, t], page[t][:, SPLIT:U])
                for lo, hi in ((0, QUANT_CUT), (QUANT_CUT, SPLIT)):
                    nc.vector.tensor_copy(grouped[0][:, lo:hi, t], page[t][:, lo:hi])
            else:
                nc.scalar.copy(grouped[0][:, :, t], page[t][:, 0:SPLIT])
                if t == FIRST:
                    h[LAST] = leave_psum("h_last", h_banks[LAST], 0, S, tag="h_late")
                nc.scalar.copy(grouped[1][:, :, t], page[t][:, SPLIT:U])

        out_words = out_1[0].rearrange("p c r -> p (c r)").bitcast(I32)
        out_plane = sb("out_plane", [P, U], U8)
        for u, lo, hi in ((0, 0, QUANT_CUT), (0, QUANT_CUT, SPLIT), (1, SPLIT, U)):
            out_codes = sb(f"out_codes{lo}", [P, hi - lo], U32)
            base = spans[u][0]
            nc.vector.quantize_mx(
                out=out_codes[:].bitcast(FP8X4), scales=out_plane[:, lo:hi],
                in_=grouped[u][:, lo - base : hi - base, :].rearrange("p n t -> p (n t)"))
            nc.sync.dma_start(out_words[:, lo:hi], out_codes[:].bitcast(I32))
        plane_rows = out_2[0].bitcast(I32)
        for q in range(QUADRANTS):
            queue = nc.scalar if q % 2 else nc.sync
            queue.dma_start(plane_rows[4 * q : 4 * q + 4, :], out_plane[32 * q : 32 * q + 4, :].bitcast(I32))
